import numpy as np
import ml_dtypes

BF16 = ml_dtypes.bfloat16


def bf(x):
    return np.asarray(x, np.float32).astype(BF16)


def f32(x):
    return np.asarray(x, np.float32)


def f64(x):
    return np.asarray(x).astype(np.float64)


def striped(idx):
    return np.tile(idx.reshape(-1, 16).T, (8, 1))


S, K, M, N, D, V = 4096, 128, 128, 3072, 2, 1536


def setup_inputs():
    return {"table": bf(np.random.standard_normal((S, K))), "w": bf(np.random.standard_normal((K, M)) / np.sqrt(D * K)), "b": f32(0.5 * np.random.standard_normal((M, 1))), "offs": striped(np.random.permutation(np.tile(np.arange(S), 2))[:N])}


def reference(table, w, b, offs):
    idx = offs[:16].T.reshape(-1)
    x = f64(table)[idx].T
    y = f64(w).T @ sum(x[:, t * V : (t + 1) * V] for t in range(D))
    return np.tanh(y + f64(b))

@@ -1,0 +1,60 @@
+import concourse.mybir as mybir
+from concourse.masks import make_identity
+
+BF16, F32, U16 = mybir.dt.bfloat16, mybir.dt.float32, mybir.dt.uint16
+
+P = 128
+NODES = 4096
+LIST = 3072
+NEIGHBOURS = 2
+OUT_COLS = LIST // NEIGHBOURS
+BANK_F32 = 512
+BANK_BF16 = 1024
+BLOCKS_PER_CHUNK = BANK_BF16 // P
+CHUNKS = NODES // BANK_BF16
+
+FLOPS = 2 * P * P * OUT_COLS + P * OUT_COLS * (NEIGHBOURS - 1)
+
+
+def tile_gather_matmul_kernel(tc, table, w, b, offs, out):
+    nc = tc.nc
+    with (
+        tc.tile_pool(name="held", bufs=1) as held,
+        tc.psum_pool(name="flip", bufs=CHUNKS) as flip,
+        tc.psum_pool(name="sums", bufs=1) as sums,
+    ):
+        offsets = held.tile([P, LIST // 16], U16, name="offsets")
+        nc.sync.dma_start(offsets[:], offs)
+
+        table_blocks = table.rearrange("(c p) k -> p c k", p=P)
+        rows = []
+        for c in range(CHUNKS):
+            chunk = held.tile([P, BLOCKS_PER_CHUNK, P], BF16, name="rows%d" % c)
+            nc.sync.dma_start(chunk[:], table_blocks[:, c * BLOCKS_PER_CHUNK : (c + 1) * BLOCKS_PER_CHUNK, :])
+            rows.append(chunk)
+
+        weights = held.tile([P, P], BF16, name="weights")
+        nc.scalar.dma_start(weights[:], w)
+        bias = held.tile([P, 1], F32, name="bias")
+        nc.scalar.dma_start(bias[:], b)
+
+        identity = held.tile([P, P], BF16, name="identity")
+        make_identity(nc, identity[:])
+
+        window = held.tile([P, NODES], BF16, name="window")
+        for c in range(CHUNKS):
+            flipped = flip.tile([P, BANK_BF16], BF16, name="flipped")
+            for j in range(BLOCKS_PER_CHUNK):
+                nc.tensor.transpose(flipped[:, j * P : (j + 1) * P], rows[c][:, j, :], identity[:])
+            nc.vector.tensor_copy(window[:, c * BANK_BF16 : (c + 1) * BANK_BF16], flipped[:])
+
+        result = held.tile([P, OUT_COLS], F32, name="result")
+        for piece in range(OUT_COLS // BANK_F32):
+            bank = sums.tile([P, BANK_F32], F32, name="bank%d" % piece)
+            for t in range(NEIGHBOURS):
+                first = (t * OUT_COLS + piece * BANK_F32) // 16
+                picked = window[:].indirect(offsets[:, first : first + BANK_F32 // 16])
+                nc.tensor.matmul(bank[:], weights[:], picked, start=(t == 0), stop=(t == NEIGHBOURS - 1))
+            cols = slice(piece * BANK_F32, (piece + 1) * BANK_F32)
+            nc.scalar.activation(result[:, cols], bank[:], mybir.ActivationFunctionType.Tanh, bias=bias[:, 0:1])
+            nc.sync.dma_start(out[:, cols], result[:, cols])

@@ -9,9 +9,9 @@ LIST = 3072
 NEIGHBOURS = 2
 OUT_COLS = LIST // NEIGHBOURS
 BANK_F32 = 512
-BANK_BF16 = 1024
-BLOCKS_PER_CHUNK = BANK_BF16 // P
-CHUNKS = NODES // BANK_BF16
+ROWS_PER_PARTITION = 4
+CHUNK = P * ROWS_PER_PARTITION
+CHUNKS = NODES // CHUNK
 
 FLOPS = 2 * P * P * OUT_COLS + P * OUT_COLS * (NEIGHBOURS - 1)
 
@@ -20,33 +20,38 @@ def tile_gather_matmul_kernel(tc, table, w, b, offs, out):
     nc = tc.nc
     with (
         tc.tile_pool(name="held", bufs=1) as held,
-        tc.psum_pool(name="flip", bufs=CHUNKS) as flip,
+        tc.psum_pool(name="flip", bufs=4) as flip,
         tc.psum_pool(name="sums", bufs=1) as sums,
     ):
         offsets = held.tile([P, LIST // 16], U16, name="offsets")
         nc.sync.dma_start(offsets[:], offs)
 
-        table_blocks = table.rearrange("(c p) k -> p c k", p=P)
+        table_chunks = table.rearrange("(c p i) k -> c p (i k)", p=P, i=ROWS_PER_PARTITION)
         rows = []
         for c in range(CHUNKS):
-            chunk = held.tile([P, BLOCKS_PER_CHUNK, P], BF16, name="rows%d" % c)
-            nc.sync.dma_start(chunk[:], table_blocks[:, c * BLOCKS_PER_CHUNK : (c + 1) * BLOCKS_PER_CHUNK, :])
+            chunk = held.tile([P, ROWS_PER_PARTITION * P], BF16, name="rows%d" % c)
+            queue = nc.sync if c % 2 == 0 else nc.scalar
+            queue.dma_start(chunk[:], table_chunks[c])
             rows.append(chunk)
-
-        weights = held.tile([P, P], BF16, name="weights")
-        nc.scalar.dma_start(weights[:], w)
-        bias = held.tile([P, 1], F32, name="bias")
-        nc.scalar.dma_start(bias[:], b)
 
         identity = held.tile([P, P], BF16, name="identity")
         make_identity(nc, identity[:])
+        weights = held.tile([P, P], BF16, name="weights")
+        nc.gpsimd.dma_start(weights[:], w)
+        bias = held.tile([P, 1], F32, name="bias")
+        nc.gpsimd.dma_start(bias[:], b)
 
         window = held.tile([P, NODES], BF16, name="window")
         for c in range(CHUNKS):
-            flipped = flip.tile([P, BANK_BF16], BF16, name="flipped")
-            for j in range(BLOCKS_PER_CHUNK):
-                nc.tensor.transpose(flipped[:, j * P : (j + 1) * P], rows[c][:, j, :], identity[:])
-            nc.vector.tensor_copy(window[:, c * BANK_BF16 : (c + 1) * BANK_BF16], flipped[:])
+            flipped = flip.tile([P, CHUNK], BF16, name="flipped")
+            for i in range(ROWS_PER_PARTITION):
+                nc.tensor.transpose(flipped[:, i * P : (i + 1) * P], rows[c][:, i * P : (i + 1) * P], identity[:])
+            in_order = flipped[:].rearrange("k (i p) -> k p i", i=ROWS_PER_PARTITION)
+            nodes = window[:, c * CHUNK : (c + 1) * CHUNK].rearrange("k (p i) -> k p i", i=ROWS_PER_PARTITION)
+            if c % 2 == 0:
+                nc.vector.tensor_copy(nodes, in_order)
+            else:
+                nc.scalar.copy(nodes, in_order)
 
         result = held.tile([P, OUT_COLS], F32, name="result")
         for piece in range(OUT_COLS // BANK_F32):

@@ -12,6 +12,7 @@ BANK_F32 = 512
 ROWS_PER_PARTITION = 4
 CHUNK = P * ROWS_PER_PARTITION
 CHUNKS = NODES // CHUNK
+WARM_UP_FIRST = 4
 
 FLOPS = 2 * P * P * OUT_COLS + P * OUT_COLS * (NEIGHBOURS - 1)
 
@@ -22,6 +23,7 @@ def tile_gather_matmul_kernel(tc, table, w, b, offs, out):
         tc.tile_pool(name="held", bufs=1) as held,
         tc.psum_pool(name="flip", bufs=4) as flip,
         tc.psum_pool(name="sums", bufs=1) as sums,
+        tc.psum_pool(name="idle", bufs=1) as idle,
     ):
         offsets = held.tile([P, LIST // 16], U16, name="offsets")
         nc.sync.dma_start(offsets[:], offs)
@@ -41,6 +43,16 @@ def tile_gather_matmul_kernel(tc, table, w, b, offs, out):
         bias = held.tile([P, 1], F32, name="bias")
         nc.gpsimd.dma_start(bias[:], b)
 
+        zeros = held.tile([P, BANK_F32], BF16, name="zeros")
+        nc.vector.memset(zeros[:], 0.0)
+        unread = idle.tile([P, BANK_F32], F32, name="unread")
+
+        def warm_up(times):
+            for turn in range(times):
+                nc.tensor.matmul(unread[:], zeros[:, 0:P], zeros[:], start=True, stop=True)
+
+        warm_up(WARM_UP_FIRST)
+
         window = held.tile([P, NODES], BF16, name="window")
         for c in range(CHUNKS):
             flipped = flip.tile([P, CHUNK], BF16, name="flipped")
@@ -52,6 +64,7 @@ def tile_gather_matmul_kernel(tc, table, w, b, offs, out):
                 nc.vector.tensor_copy(nodes, in_order)
             else:
                 nc.scalar.copy(nodes, in_order)
+                warm_up(1)
 
         result = held.tile([P, OUT_COLS], F32, name="result")
         for piece in range(OUT_COLS // BANK_F32):

@@ -2,6 +2,7 @@ import concourse.mybir as mybir
 from concourse.masks import make_identity
 
 BF16, F32, U16 = mybir.dt.bfloat16, mybir.dt.float32, mybir.dt.uint16
+TANH = mybir.ActivationFunctionType.Tanh
 
 P = 128
 NODES = 4096
@@ -9,10 +10,12 @@ LIST = 3072
 NEIGHBOURS = 2
 OUT_COLS = LIST // NEIGHBOURS
 BANK_F32 = 512
+HALF = BANK_F32 // 2
 ROWS_PER_PARTITION = 4
 CHUNK = P * ROWS_PER_PARTITION
 CHUNKS = NODES // CHUNK
-WARM_UP_FIRST = 4
+IDLE_COLS = 256
+IDLE_MATMULS = 8
 
 FLOPS = 2 * P * P * OUT_COLS + P * OUT_COLS * (NEIGHBOURS - 1)
 
@@ -25,46 +28,42 @@ def tile_gather_matmul_kernel(tc, table, w, b, offs, out):
         tc.psum_pool(name="sums", bufs=1) as sums,
         tc.psum_pool(name="idle", bufs=1) as idle,
     ):
-        offsets = held.tile([P, LIST // 16], U16, name="offsets")
-        nc.sync.dma_start(offsets[:], offs)
-
-        table_chunks = table.rearrange("(c p i) k -> c p (i k)", p=P, i=ROWS_PER_PARTITION)
+        table_chunks = table.rearrange("(c i p) k -> c p i k", p=P, i=ROWS_PER_PARTITION)
         rows = []
         for c in range(CHUNKS):
             chunk = held.tile([P, ROWS_PER_PARTITION * P], BF16, name="rows%d" % c)
             queue = nc.sync if c % 2 == 0 else nc.scalar
-            queue.dma_start(chunk[:], table_chunks[c])
+            queue.dma_start(chunk[:].rearrange("p (i k) -> p i k", i=ROWS_PER_PARTITION), table_chunks[c])
             rows.append(chunk)
 
+        offsets = held.tile([P, LIST // 16], U16, name="offsets")
+        nc.sync.dma_start(offsets[:], offs)
+        weights = held.tile([P, P], BF16, name="weights")
+        nc.sync.dma_start(weights[:], w)
+        bias = held.tile([P, 1], F32, name="bias")
+        nc.sync.dma_start(bias[:], b)
         identity = held.tile([P, P], BF16, name="identity")
         make_identity(nc, identity[:])
-        weights = held.tile([P, P], BF16, name="weights")
-        nc.gpsimd.dma_start(weights[:], w)
-        bias = held.tile([P, 1], F32, name="bias")
-        nc.gpsimd.dma_start(bias[:], b)
 
-        zeros = held.tile([P, BANK_F32], BF16, name="zeros")
+        zeros = held.tile([P, IDLE_COLS], BF16, name="zeros")
         nc.vector.memset(zeros[:], 0.0)
-        unread = idle.tile([P, BANK_F32], F32, name="unread")
+        unread = idle.tile([P, IDLE_COLS], F32, name="unread")
+        for turn in range(IDLE_MATMULS):
+            nc.tensor.matmul(unread[:], zeros[:, 0:P], zeros[:], start=True, stop=True)
 
-        def warm_up(times):
-            for turn in range(times):
-                nc.tensor.matmul(unread[:], zeros[:, 0:P], zeros[:], start=True, stop=True)
-
-        warm_up(WARM_UP_FIRST)
+        unused = held.tile([P, 1], F32, name="unused")
+        nc.scalar.activation(unused[:], zeros[:, 0:1], TANH)
 
         window = held.tile([P, NODES], BF16, name="window")
         for c in range(CHUNKS):
             flipped = flip.tile([P, CHUNK], BF16, name="flipped")
             for i in range(ROWS_PER_PARTITION):
                 nc.tensor.transpose(flipped[:, i * P : (i + 1) * P], rows[c][:, i * P : (i + 1) * P], identity[:])
-            in_order = flipped[:].rearrange("k (i p) -> k p i", i=ROWS_PER_PARTITION)
-            nodes = window[:, c * CHUNK : (c + 1) * CHUNK].rearrange("k (p i) -> k p i", i=ROWS_PER_PARTITION)
+            columns = window[:, c * CHUNK : (c + 1) * CHUNK]
             if c % 2 == 0:
-                nc.vector.tensor_copy(nodes, in_order)
+                nc.scalar.copy(columns, flipped[:])
             else:
-                nc.scalar.copy(nodes, in_order)
-                warm_up(1)
+                nc.vector.tensor_copy(columns, flipped[:])
 
         result = held.tile([P, OUT_COLS], F32, name="result")
         for piece in range(OUT_COLS // BANK_F32):
@@ -73,6 +72,8 @@ def tile_gather_matmul_kernel(tc, table, w, b, offs, out):
                 first = (t * OUT_COLS + piece * BANK_F32) // 16
                 picked = window[:].indirect(offsets[:, first : first + BANK_F32 // 16])
                 nc.tensor.matmul(bank[:], weights[:], picked, start=(t == 0), stop=(t == NEIGHBOURS - 1))
-            cols = slice(piece * BANK_F32, (piece + 1) * BANK_F32)
-            nc.scalar.activation(result[:, cols], bank[:], mybir.ActivationFunctionType.Tanh, bias=bias[:, 0:1])
-            nc.sync.dma_start(out[:, cols], result[:, cols])
+            for half in range(2):
+                in_bank = slice(half * HALF, (half + 1) * HALF)
+                cols = slice(piece * BANK_F32 + half * HALF, piece * BANK_F32 + (half + 1) * HALF)
+                nc.scalar.activation(result[:, cols], bank[:, in_bank], TANH, bias=bias[:, 0:1])
+                nc.sync.dma_start(out[:, cols], result[:, cols])

import concourse.mybir as mybir
from concourse.masks import make_identity

BF16, F32, U16 = mybir.dt.bfloat16, mybir.dt.float32, mybir.dt.uint16
TANH = mybir.ActivationFunctionType.Tanh

P = 128
NODES = 4096
LIST = 3072
NEIGHBOURS = 2
OUT_COLS = LIST // NEIGHBOURS
BANK_F32 = 512
HALF = BANK_F32 // 2
ROWS_PER_PARTITION = 4
CHUNK = P * ROWS_PER_PARTITION
CHUNKS = NODES // CHUNK
IDLE_COLS = 256
IDLE_MATMULS = 8

FLOPS = 2 * P * P * OUT_COLS + P * OUT_COLS * (NEIGHBOURS - 1)


def tile_gather_matmul_kernel(tc, table, w, b, offs, out):
    nc = tc.nc
    with (
        tc.tile_pool(name="held", bufs=1) as held,
        tc.psum_pool(name="flip", bufs=4) as flip,
        tc.psum_pool(name="sums", bufs=1) as sums,
        tc.psum_pool(name="idle", bufs=1) as idle,
    ):
        table_chunks = table.rearrange("(c i p) k -> c p i k", p=P, i=ROWS_PER_PARTITION)
        rows = []
        for c in range(CHUNKS):
            chunk = held.tile([P, ROWS_PER_PARTITION * P], BF16, name="rows%d" % c)
            queue = nc.sync if c % 2 == 0 else nc.scalar
            queue.dma_start(chunk[:].rearrange("p (i k) -> p i k", i=ROWS_PER_PARTITION), table_chunks[c])
            rows.append(chunk)

        offsets = held.tile([P, LIST // 16], U16, name="offsets")
        nc.sync.dma_start(offsets[:], offs)
        weights = held.tile([P, P], BF16, name="weights")
        nc.sync.dma_start(weights[:], w)
        bias = held.tile([P, 1], F32, name="bias")
        nc.sync.dma_start(bias[:], b)
        identity = held.tile([P, P], BF16, name="identity")
        make_identity(nc, identity[:])

        zeros = held.tile([P, IDLE_COLS], BF16, name="zeros")
        nc.vector.memset(zeros[:], 0.0)
        unread = idle.tile([P, IDLE_COLS], F32, name="unread")
        for turn in range(IDLE_MATMULS):
            nc.tensor.matmul(unread[:], zeros[:, 0:P], zeros[:], start=True, stop=True)

        unused = held.tile([P, 1], F32, name="unused")
        nc.scalar.activation(unused[:], zeros[:, 0:1], TANH)

        window = held.tile([P, NODES], BF16, name="window")
        for c in range(CHUNKS):
            flipped = flip.tile([P, CHUNK], BF16, name="flipped")
            for i in range(ROWS_PER_PARTITION):
                nc.tensor.transpose(flipped[:, i * P : (i + 1) * P], rows[c][:, i * P : (i + 1) * P], identity[:])
            columns = window[:, c * CHUNK : (c + 1) * CHUNK]
            if c % 2 == 0:
                nc.scalar.copy(columns, flipped[:])
            else:
                nc.vector.tensor_copy(columns, flipped[:])

        result = held.tile([P, OUT_COLS], F32, name="result")
        for piece in range(OUT_COLS // BANK_F32):
            bank = sums.tile([P, BANK_F32], F32, name="bank%d" % piece)
            for t in range(NEIGHBOURS):
                first = (t * OUT_COLS + piece * BANK_F32) // 16
                picked = window[:].indirect(offsets[:, first : first + BANK_F32 // 16])
                nc.tensor.matmul(bank[:], weights[:], picked, start=(t == 0), stop=(t == NEIGHBOURS - 1))
            for half in range(2):
                in_bank = slice(half * HALF, (half + 1) * HALF)
                cols = slice(piece * BANK_F32 + half * HALF, piece * BANK_F32 + (half + 1) * HALF)
                nc.scalar.activation(result[:, cols], bank[:, in_bank], TANH, bias=bias[:, 0:1])
                nc.sync.dma_start(out[:, cols], result[:, cols])
